import numpy as np
import ml_dtypes


def mxq(x, axis, fmt="e4m3"):
    dtype, down = {"e4m3": (ml_dtypes.float8_e4m3fn, 7), "e5m2": (ml_dtypes.float8_e5m2, 14)}[fmt]
    v = np.moveaxis(np.asarray(x, np.float32).astype(ml_dtypes.bfloat16).astype(np.float64), axis, -1)
    blocks = v.reshape(v.shape[:-1] + (-1, 32))
    amax = np.abs(blocks).max(-1, keepdims=True)
    byte = np.maximum(np.where(amax > 0, np.frexp(amax)[1] - 1 + 127, 0) - down, 1)
    scale = np.exp2(byte - 127.0)
    codes = (blocks / scale).astype(np.float32).astype(dtype).astype(np.float64)
    return np.moveaxis((codes * scale).reshape(v.shape), -1, axis)


WIDE = False


def mx_kscale(k):
    if not WIDE:
        return np.ones(k)
    levels = np.array([10, -10, 5, -5, 0])
    if k % 512:
        return np.exp2(np.random.permutation(np.resize(levels, k // 32))).repeat(32)
    a = np.empty((k // 512, 16))
    for p in range(k // 512):
        a[p, :8] = np.random.permutation(np.resize(levels, 8))
        for g in range(8):
            far = levels[np.abs(levels - a[p, g]) >= 10]
            a[p, g + 8] = far[np.random.randint(len(far))]
    return np.exp2(a.ravel()).repeat(32)


BF16 = ml_dtypes.bfloat16


def bf(x):
    return np.asarray(x, np.float32).astype(BF16)


def f64(x):
    return np.asarray(x).astype(np.float64)


E2M1 = np.array([0.0, 0.5, 1.0, 1.5, 2.0, 3.0, 4.0, 6.0, -0.0, -0.5, -1.0, -1.5, -2.0, -3.0, -4.0, -6.0])


def pack_weight(w, fmt):
    k, n = w.shape
    w = f64(bf(w)).reshape(k // 32, 32, n)
    amax = np.abs(w).max(1)
    if fmt == "e4m3":
        byte = np.frexp(amax)[1] - 1 + 127 - 7
    else:
        mant, ex = np.frexp(amax / 6.0)
        byte = np.where(mant > 0.5, ex, ex - 1) + 127
    byte = np.clip(np.where(amax > 0, byte, 1), 1, 254)
    scaled = (w * np.exp2(127.0 - byte)[:, None, :]).reshape(k, n).astype(np.float32)
    by_word = np.ascontiguousarray(scaled.reshape(k // 512, 128, 4, n).transpose(0, 1, 3, 2))
    if fmt == "e4m3":
        words = by_word.astype(ml_dtypes.float8_e4m3fn).view(np.uint8)
    else:
        c = by_word.astype(ml_dtypes.float4_e2m1fn).view(np.uint8) & 0xF
        words = c[..., 0::2] | (c[..., 1::2] << 4)
    return np.ascontiguousarray(words), np.ascontiguousarray(byte.astype(np.uint8).reshape(k // 512, 16, n))


def unpack_weight(words, scales, fmt):
    g, p, n, _ = words.shape
    if fmt == "e4m3":
        vals = np.ascontiguousarray(words).view(ml_dtypes.float8_e4m3fn).astype(np.float64)
    else:
        nib = np.empty((g, p, n, 4), np.uint8)
        nib[..., 0::2] = words & 0xF
        nib[..., 1::2] = words >> 4
        vals = E2M1[nib]
    vals = vals * np.repeat(np.exp2(scales.astype(np.float64) - 127.0), 8, axis=1)[..., None]
    return vals.transpose(0, 1, 3, 2).reshape(g * 512, n)
def pack4(w):
    words, scales = pack_weight(w, "e2m1")
    return words.reshape(words.shape[0], 128, -1), scales


def unpack4(words, scales):
    return unpack_weight(words.reshape(words.shape[0], 128, -1, 2), scales, "e2m1")


def planes(Y):
    n, m = Y.shape
    b = f64(bf(Y)).reshape(n // 32, 32, m)
    amax = np.abs(b).max(1)
    byte = np.clip(np.where(amax > 0, np.frexp(amax)[1] - 1 + 127 - 7, 1), 1, 254)
    codes = (b * np.exp2(127.0 - byte)[:, None, :]).reshape(n, m).astype(np.float32).astype(ml_dtypes.float8_e4m3fn).view(np.uint8)
    words = codes.reshape(n // 512, 128, 4, m).transpose(0, 1, 3, 2)
    return np.ascontiguousarray(words), np.ascontiguousarray(byte.astype(np.uint8).reshape(n // 512, 16, m))


D = 1024

KAPPA = D * D / 32
COEF = 8 * KAPPA / (D * D)


def setup_inputs():
    row = np.exp(0.5 * np.random.randn(D, 1))
    col = np.exp(0.3 * np.random.randn(1, D))
    draw = 0.7 * row * col * np.random.randn(D, D)
    eye = np.eye(D)
    w = bf(np.where(eye > 0, 0.0, draw))
    a = f64(w) ** 2
    s = mx_kscale(D)
    t = mx_kscale(D)
    u_words, u_scales = pack4((a * s[None, :]).T)
    v_words, v_scales = pack4(a / D / s[:, None] * t[None, :])
    lin = bf((D * eye + 2 * a) * t[None, :])
    m1 = bf((eye + a / D) / t[:, None])
    return {"u_words": u_words, "u_scales": u_scales, "v_words": v_words, "v_scales": v_scales,
            "lin": lin, "m1": m1, "w": w}


def reference(u_words, u_scales, v_words, v_scales, lin, m1, w):
    u = unpack4(u_words, u_scales)
    v = unpack4(v_words, v_scales)
    p = (u.T @ v) + f64(lin)
    z = mxq(p, 1, "e4m3") @ mxq(f64(m1), 0, "e4m3")
    y = z.T * f64(w) * COEF
    Y = y.reshape(D, D)
    words, scales = planes(Y)
    return y, words, scales

@@ -1,0 +1,188 @@
+from contextlib import ExitStack
+
+import concourse.mybir as mybir
+from concourse.masks import make_identity
+
+F32 = mybir.dt.float32
+BF16 = mybir.dt.bfloat16
+I32 = mybir.dt.int32
+U32 = mybir.dt.uint32
+U8 = mybir.dt.uint8
+FP8X4 = mybir.dt.float8_e4m3fn_x4
+FP4X4 = mybir.dt.float4_e2m1fn_x4
+ALU = mybir.AluOpType
+
+D = 1024
+FLOPS = 2 * 2 * D * D * D
+COEF = 0.25
+ORDER = "ms U0 sc0 sc1 sc2 sc3 sc4 sc5 V0 sc6 sc7 M00 V1 L0 L1 M10 L2 L3 U1 s1_00 L4 iM000 M01 s1_01 L5 ad00 iM001 s1_10 L6 ad01 s1_11 ad10 s1_20 ad11 W00 iM100 s1_21 qM00 M11 s1_30 ad20 L7 iM101 s1_31 ad21 W10 tr0 ad30 W01 tr1 cp0 ad31 s1_40 cp1 qM10 s1_41 W11 iM010 ad40 tr2 ad41 tr3 s1_50 qP0 cp2 s1_51 cp3 ad50 s1_60 iM011 ad51 s1_61 qP1 s2_000 ad60 iM110 s2_001 ad61 tr4 qM01 tr5 iM111 mu000 s2_100 mu001 s2_101 cp4 mu100 sy00 s1_70 cp5 mu101 s1_71 iY00 qM11 sy10 ad70 s2_010 ad71 iY10 s2_011 mu010 s2_110 mu011 s2_111 qP2 sy01 tr6 qY00 tr7 cp6 mu110 s2_200 cp7 mu111 s2_201 iY01 qY10 sy11 mu200 s2_210 mu201 s2_211 iY11 qP3 qY01 s2_300 mu210 sq0 sy20 iY20 s2_301 mu211 s2_310 qY11 sy21 mu300 sq1 s2_311 iY21 mu301 qY20 sy30 mu310 iY30 mu311 qY21 sy31 iY31 sq2 qY30 qY31 ss0 ss1 ss2 ss3 sq3".split()
+ON_VECTOR = ["iY31"]
+ON_GPSIMD = []
+
+
+def tile_notears_acyclicity_gradient_k5_kernel(tc, u_words, u_scales, v_words, v_scales, lin, m1, w, out_0, out_1, out_2):
+    nc = tc.nc
+    with ExitStack() as ctx:
+        sb = ctx.enter_context(tc.tile_pool(name="sb", bufs=1))
+        acc_pool = ctx.enter_context(tc.psum_pool(name="acc", bufs=6))
+        turn_pool = ctx.enter_context(tc.psum_pool(name="turn", bufs=2))
+
+        def tiles(name, n, shape, dtype):
+            return [sb.tile(shape, dtype, name="%s%d" % (name, j), align_bytes=64) for j in range(n)]
+
+        ident = sb.tile([128, 128], F32, name="ident", align_bytes=64)
+        uv_sc = sb.tile([128, 2, 2, D], U8, name="uv_sc", align_bytes=64)
+        u_sb = tiles("u_sb", 2, [128, 2, 1024], U8)
+        v_sb = tiles("v_sb", 2, [128, 2, 1024], U8)
+        l_sb = tiles("l_sb", 8, [128, D], BF16)
+        m_raw = tiles("m_raw", 4, [128, 4, 512], BF16)
+        m_int = tiles("m_int", 4, [128, 2048], BF16)
+        m_codes = tiles("m_codes", 4, [128, 512], U32)
+        m_sc = tiles("m_sc", 4, [128, 512], U8)
+        w_sb = tiles("w_sb", 4, [128, 4, 512], BF16)
+        p_nat = tiles("p_nat", 8, [128, D], BF16)
+        p_t = tiles("p_t", 4, [128, 2048], BF16)
+        p_codes = tiles("p_codes", 4, [128, 2, 256], U32)
+        p_sc = tiles("p_sc", 4, [128, 2, 256], U8)
+        y_sb = tiles("y_sb", 8, [128, 4, 256], F32)
+        y_int = tiles("y_int", 8, [128, 1024], BF16)
+        y_codes = tiles("y_codes", 4, [128, 2, 256], U32)
+        y_sc = sb.tile([128, 2, D], U8, name="y_sc", align_bytes=64)
+        banks = {}
+
+        def move(name, out, in_):
+            if name in ON_VECTOR:
+                nc.vector.tensor_copy(out=out, in_=in_)
+            elif name in ON_GPSIMD:
+                nc.gpsimd.tensor_scalar(out=out, in0=in_, scalar1=1.0, scalar2=0.0, op0=ALU.mult, op1=ALU.add)
+            else:
+                nc.scalar.copy(out=out, in_=in_)
+
+        def emit(name):
+            if name == "ms":
+                nc.vector.memset(uv_sc[:].rearrange("p o g n -> p (o g n)").bitcast(I32), 0)
+                make_identity(nc, ident[:])
+            elif name.startswith("sc"):
+                o, q = divmod(int(name[2]), 4)
+                src = (u_scales, v_scales)[o]
+                nc.sync.dma_start(
+                    out=uv_sc[32 * q : 32 * q + 4, o, :, :].bitcast(I32),
+                    in_=src[:, 4 * q : 4 * q + 4, :].rearrange("g r n -> r g n").bitcast(I32))
+            elif name[0] in "UV":
+                h = int(name[1])
+                src, dst = (u_words, u_sb) if name[0] == "U" else (v_words, v_sb)
+                nc.sync.dma_start(
+                    out=dst[h][:].bitcast(I32),
+                    in_=src[:, :, 1024 * h : 1024 * h + 1024].rearrange("g p n -> p g n").bitcast(I32))
+            elif name[0] == "L":
+                a = int(name[1])
+                nc.sync.dma_start(out=l_sb[a][:], in_=lin[128 * a : 128 * a + 128, :])
+            elif name[0] == "M":
+                k, g = int(name[1]), int(name[2])
+                nc.sync.dma_start(
+                    out=m_raw[2 * k + g][:],
+                    in_=m1[512 * k : 512 * k + 512, 512 * g : 512 * g + 512].rearrange("(p j) c -> p j c", j=4))
+            elif name[0] == "W":
+                g, h = int(name[1]), int(name[2])
+                nc.sync.dma_start(
+                    out=w_sb[2 * g + h][:],
+                    in_=w[512 * g : 512 * g + 512, 512 * h : 512 * h + 512].rearrange("(p t) a -> p t a", t=4))
+            elif name.startswith("iM"):
+                k, g, hh = int(name[2]), int(name[3]), int(name[4])
+                ms = slice(64 * hh, 64 * hh + 64)
+                move(name,
+                     m_int[2 * k + g][:].rearrange("p (t m j) -> p m j t", t=4, j=4)[:, ms],
+                     m_raw[2 * k + g][:].rearrange("p j (m t) -> p m j t", t=4)[:, ms])
+            elif name.startswith("qM"):
+                k, g = int(name[2]), int(name[3])
+                nc.vector.quantize_mx(out=m_codes[2 * k + g][:].bitcast(FP8X4), scales=m_sc[2 * k + g][:], in_=m_int[2 * k + g][:])
+            elif name.startswith("s1_"):
+                a, h = int(name[3]), int(name[4])
+                bank = acc_pool.tile([128, 512], F32, name="acc")
+                banks[name] = bank
+                for g in range(2):
+                    nc.tensor.matmul_mx(
+                        out=bank[:],
+                        lhsT=u_sb[a // 4][:, g, 256 * (a % 4) : 256 * (a % 4) + 256].bitcast(FP4X4),
+                        lhsT_scale=uv_sc[:, 0, g, 128 * a : 128 * a + 128],
+                        rhs=v_sb[h][:, g, :].bitcast(FP4X4),
+                        rhs_scale=uv_sc[:, 1, g, 512 * h : 512 * h + 512],
+                        start=(g == 0), stop=(g == 1))
+            elif name.startswith("ad"):
+                a, h = int(name[2]), int(name[3])
+                cols = slice(512 * h, 512 * h + 512)
+                nc.vector.tensor_tensor(
+                    out=p_nat[a][:, cols].rearrange("a (u q e) -> a u q e", u=2, e=2),
+                    in0=banks["s1_%d%d" % (a, h)][:].rearrange("a (q u e) -> a u q e", u=2, e=2),
+                    in1=l_sb[a][:, cols].rearrange("a (q u e) -> a u q e", u=2, e=2),
+                    op=ALU.add)
+            elif name.startswith("tr"):
+                a = int(name[2])
+                bank = turn_pool.tile([128, 4, 128], F32, name="turn")
+                banks[name] = bank
+                words = p_nat[a][:].bitcast(F32)
+                for s in range(4):
+                    nc.tensor.transpose(bank[:, s, :], words[:, 128 * s : 128 * s + 128], ident[:])
+            elif name.startswith("cp"):
+                a = int(name[2])
+                nc.scalar.copy(
+                    out=p_t[a // 2][:].bitcast(F32).rearrange("p (k a u) -> p k a u", k=2, u=2)[:, :, 128 * (a % 2) : 128 * (a % 2) + 128, :],
+                    in_=banks["tr%d" % a][:].rearrange("p (k u) a -> p k a u", k=2))
+            elif name.startswith("qP"):
+                i = int(name[2])
+                nc.vector.quantize_mx(
+                    out=p_codes[i][:].rearrange("p k a -> p (k a)").bitcast(FP8X4),
+                    scales=p_sc[i][:].rearrange("p k a -> p (k a)"), in_=p_t[i][:])
+            elif name.startswith("s2_"):
+                i, g, b = int(name[3]), int(name[4]), int(name[5])
+                bank = acc_pool.tile([128, 512], F32, name="acc")
+                banks[name] = bank
+                for tt in range(2):
+                    t = 2 * b + tt
+                    for k in range(2):
+                        nc.tensor.matmul_mx(
+                            out=bank[:, 256 * tt : 256 * tt + 256],
+                            lhsT=m_codes[2 * k + g][:, 128 * t : 128 * t + 128].bitcast(FP8X4),
+                            lhsT_scale=m_sc[2 * k + g][:, 128 * t : 128 * t + 128],
+                            rhs=p_codes[i][:, k, :].bitcast(FP8X4),
+                            rhs_scale=p_sc[i][:, k, :],
+                            start=(k == 0), stop=(k == 1))
+            elif name.startswith("mu"):
+                i, g, b = int(name[2]), int(name[3]), int(name[4])
+                nc.vector.scalar_tensor_tensor(
+                    out=y_sb[2 * i + g][:, 2 * b : 2 * b + 2, :],
+                    in0=banks["s2_%d%d%d" % (i, g, b)][:].rearrange("p (t a) -> p t a", t=2),
+                    scalar=COEF,
+                    in1=w_sb[2 * g + i // 2][:, 2 * b : 2 * b + 2, 256 * (i % 2) : 256 * (i % 2) + 256],
+                    op0=ALU.mult, op1=ALU.mult)
+            elif name.startswith("iY"):
+                i, g = int(name[2]), int(name[3])
+                move(name,
+                     y_int[2 * i + g][:].rearrange("p (c i t) -> p c t i", i=4, t=4),
+                     y_sb[2 * i + g][:].rearrange("p t (c i) -> p c t i", i=4))
+            elif name.startswith("qY"):
+                i, g = int(name[2]), int(name[3])
+                nc.vector.quantize_mx(
+                    out=y_codes[i][:, g, :].bitcast(FP8X4),
+                    scales=y_sc[:, g, 256 * i : 256 * i + 256], in_=y_int[2 * i + g][:])
+            elif name.startswith("sy"):
+                i, g = int(name[2]), int(name[3])
+                nc.sync.dma_start(
+                    out=out_0[512 * g : 512 * g + 512, 256 * i : 256 * i + 256].rearrange("(p t) a -> p t a", t=4),
+                    in_=y_sb[2 * i + g][:])
+            elif name.startswith("sq"):
+                i = int(name[2])
+                nc.sync.dma_start(
+                    out=out_1.rearrange("g p m t -> p g (m t)")[:, :, 1024 * i : 1024 * i + 1024].bitcast(I32),
+                    in_=y_codes[i][:].bitcast(I32))
+            elif name.startswith("ss"):
+                q = int(name[2])
+                nc.sync.dma_start(
+                    out=out_2[:, 4 * q : 4 * q + 4, :].rearrange("g r n -> r g n").bitcast(I32),
+                    in_=y_sc[32 * q : 32 * q + 4, :, :].bitcast(I32))
+            else:
+                raise ValueError(name)
+
+        with tc.manual_schedule():
+            for name in ORDER:
+                emit(name)

@@ -13,176 +13,281 @@ FP4X4 = mybir.dt.float4_e2m1fn_x4
 ALU = mybir.AluOpType
 
 D = 1024
-FLOPS = 2 * 2 * D * D * D
+P = 128
+PACK = 4
+GROUP = P * PACK
+BLOCK = 256
 COEF = 0.25
-ORDER = "ms U0 sc0 sc1 sc2 sc3 sc4 sc5 V0 sc6 sc7 M00 V1 L0 L1 M10 L2 L3 U1 s1_00 L4 iM000 M01 s1_01 L5 ad00 iM001 s1_10 L6 ad01 s1_11 ad10 s1_20 ad11 W00 iM100 s1_21 qM00 M11 s1_30 ad20 L7 iM101 s1_31 ad21 W10 tr0 ad30 W01 tr1 cp0 ad31 s1_40 cp1 qM10 s1_41 W11 iM010 ad40 tr2 ad41 tr3 s1_50 qP0 cp2 s1_51 cp3 ad50 s1_60 iM011 ad51 s1_61 qP1 s2_000 ad60 iM110 s2_001 ad61 tr4 qM01 tr5 iM111 mu000 s2_100 mu001 s2_101 cp4 mu100 sy00 s1_70 cp5 mu101 s1_71 iY00 qM11 sy10 ad70 s2_010 ad71 iY10 s2_011 mu010 s2_110 mu011 s2_111 qP2 sy01 tr6 qY00 tr7 cp6 mu110 s2_200 cp7 mu111 s2_201 iY01 qY10 sy11 mu200 s2_210 mu201 s2_211 iY11 qP3 qY01 s2_300 mu210 sq0 sy20 iY20 s2_301 mu211 s2_310 qY11 sy21 mu300 sq1 s2_311 iY21 mu301 qY20 sy30 mu310 iY30 mu311 qY21 sy31 iY31 sq2 qY30 qY31 ss0 ss1 ss2 ss3 sq3".split()
-ON_VECTOR = ["iY31"]
-ON_GPSIMD = []
+FLOPS = 2 * 2 * D * D * D
+
+SUM_BANKS = 6
+TURN_BANKS = 2
+WARM_PASSES = 4
 
 
-def tile_notears_acyclicity_gradient_k5_kernel(tc, u_words, u_scales, v_words, v_scales, lin, m1, w, out_0, out_1, out_2):
+def tile_notears_acyclicity_gradient_k5_kernel(
+    tc, u_words, u_scales, v_words, v_scales, lin, m1, w, out_0, out_1, out_2
+):
     nc = tc.nc
     with ExitStack() as ctx:
-        sb = ctx.enter_context(tc.tile_pool(name="sb", bufs=1))
-        acc_pool = ctx.enter_context(tc.psum_pool(name="acc", bufs=6))
-        turn_pool = ctx.enter_context(tc.psum_pool(name="turn", bufs=2))
+        sbuf = ctx.enter_context(tc.tile_pool(name="sbuf", bufs=1))
+        sum_pool = ctx.enter_context(tc.psum_pool(name="sums", bufs=SUM_BANKS))
+        turn_pool = ctx.enter_context(tc.psum_pool(name="turns", bufs=TURN_BANKS))
 
-        def tiles(name, n, shape, dtype):
-            return [sb.tile(shape, dtype, name="%s%d" % (name, j), align_bytes=64) for j in range(n)]
+        def tile(name, shape, dtype):
+            return sbuf.tile(shape, dtype, name=name, align_bytes=64)
 
-        ident = sb.tile([128, 128], F32, name="ident", align_bytes=64)
-        uv_sc = sb.tile([128, 2, 2, D], U8, name="uv_sc", align_bytes=64)
-        u_sb = tiles("u_sb", 2, [128, 2, 1024], U8)
-        v_sb = tiles("v_sb", 2, [128, 2, 1024], U8)
-        l_sb = tiles("l_sb", 8, [128, D], BF16)
-        m_raw = tiles("m_raw", 4, [128, 4, 512], BF16)
-        m_int = tiles("m_int", 4, [128, 2048], BF16)
-        m_codes = tiles("m_codes", 4, [128, 512], U32)
-        m_sc = tiles("m_sc", 4, [128, 512], U8)
-        w_sb = tiles("w_sb", 4, [128, 4, 512], BF16)
-        p_nat = tiles("p_nat", 8, [128, D], BF16)
-        p_t = tiles("p_t", 4, [128, 2048], BF16)
-        p_codes = tiles("p_codes", 4, [128, 2, 256], U32)
-        p_sc = tiles("p_sc", 4, [128, 2, 256], U8)
-        y_sb = tiles("y_sb", 8, [128, 4, 256], F32)
-        y_int = tiles("y_int", 8, [128, 1024], BF16)
-        y_codes = tiles("y_codes", 4, [128, 2, 256], U32)
-        y_sc = sb.tile([128, 2, D], U8, name="y_sc", align_bytes=64)
-        banks = {}
+        def tiles(name, count, shape, dtype):
+            return [tile("%s%d" % (name, j), shape, dtype) for j in range(count)]
 
-        def move(name, out, in_):
-            if name in ON_VECTOR:
-                nc.vector.tensor_copy(out=out, in_=in_)
-            elif name in ON_GPSIMD:
-                nc.gpsimd.tensor_scalar(out=out, in0=in_, scalar1=1.0, scalar2=0.0, op0=ALU.mult, op1=ALU.add)
-            else:
-                nc.scalar.copy(out=out, in_=in_)
+        ident = tile("ident", [P, P], F32)
+        u_scale = tile("u_scale", [P, 2, D], U8)
+        v_scale = tile("v_scale", [P, 2, D], U8)
+        u_half = tiles("u_half", 2, [P, 2, 2 * GROUP], U8)
+        v_half = tiles("v_half", 2, [P, 2, 2 * GROUP], U8)
+        warm_in = tile("warm_in", [P, PACK * GROUP], BF16)
+        warm_codes = tile("warm_codes", [P, GROUP], U32)
+        warm_scale = tile("warm_scale", [P, GROUP], U8)
+        l_rows = tiles("l_rows", D // P, [P, D], BF16)
+        p_rows = tiles("p_rows", D // P, [P, D], BF16)
+        p_inter = tiles("p_inter", D // BLOCK, [P, 2 * BLOCK * PACK], BF16)
+        p_codes = tiles("p_codes", D // BLOCK, [P, 2, BLOCK], U32)
+        p_scale = tiles("p_scale", D // BLOCK, [P, 2, BLOCK], U8)
+        m_raw = tiles("m_raw", 4, [P, PACK, GROUP], BF16)
+        m_inter = tiles("m_inter", 4, [P, PACK * GROUP], BF16)
+        m_codes = tiles("m_codes", 4, [P, GROUP], U32)
+        m_scale = tiles("m_scale", 4, [P, GROUP], U8)
+        w_rows = tiles("w_rows", 2, [P, PACK, D], BF16)
+        y_rows = tiles("y_rows", 2, [P, PACK, D], F32)
+        y_inter = tiles("y_inter", 2, [P, PACK * D], BF16)
+        y_codes = tiles("y_codes", 2, [P, D], U32)
+        y_scale = tile("y_scale", [P, 2, D], U8)
 
-        def emit(name):
-            if name == "ms":
-                nc.vector.memset(uv_sc[:].rearrange("p o g n -> p (o g n)").bitcast(I32), 0)
-                make_identity(nc, ident[:])
-            elif name.startswith("sc"):
-                o, q = divmod(int(name[2]), 4)
-                src = (u_scales, v_scales)[o]
-                nc.sync.dma_start(
-                    out=uv_sc[32 * q : 32 * q + 4, o, :, :].bitcast(I32),
-                    in_=src[:, 4 * q : 4 * q + 4, :].rearrange("g r n -> r g n").bitcast(I32))
-            elif name[0] in "UV":
-                h = int(name[1])
-                src, dst = (u_words, u_sb) if name[0] == "U" else (v_words, v_sb)
-                nc.sync.dma_start(
-                    out=dst[h][:].bitcast(I32),
-                    in_=src[:, :, 1024 * h : 1024 * h + 1024].rearrange("g p n -> p g n").bitcast(I32))
-            elif name[0] == "L":
-                a = int(name[1])
-                nc.sync.dma_start(out=l_sb[a][:], in_=lin[128 * a : 128 * a + 128, :])
-            elif name[0] == "M":
-                k, g = int(name[1]), int(name[2])
-                nc.sync.dma_start(
-                    out=m_raw[2 * k + g][:],
-                    in_=m1[512 * k : 512 * k + 512, 512 * g : 512 * g + 512].rearrange("(p j) c -> p j c", j=4))
-            elif name[0] == "W":
-                g, h = int(name[1]), int(name[2])
-                nc.sync.dma_start(
-                    out=w_sb[2 * g + h][:],
-                    in_=w[512 * g : 512 * g + 512, 512 * h : 512 * h + 512].rearrange("(p t) a -> p t a", t=4))
-            elif name.startswith("iM"):
-                k, g, hh = int(name[2]), int(name[3]), int(name[4])
-                ms = slice(64 * hh, 64 * hh + 64)
-                move(name,
-                     m_int[2 * k + g][:].rearrange("p (t m j) -> p m j t", t=4, j=4)[:, ms],
-                     m_raw[2 * k + g][:].rearrange("p j (m t) -> p m j t", t=4)[:, ms])
-            elif name.startswith("qM"):
-                k, g = int(name[2]), int(name[3])
-                nc.vector.quantize_mx(out=m_codes[2 * k + g][:].bitcast(FP8X4), scales=m_sc[2 * k + g][:], in_=m_int[2 * k + g][:])
-            elif name.startswith("s1_"):
-                a, h = int(name[3]), int(name[4])
-                bank = acc_pool.tile([128, 512], F32, name="acc")
-                banks[name] = bank
-                for g in range(2):
+        def span(index, width, count=1):
+            return slice(index * width, (index + count) * width)
+
+        def load_scale_rows(plane, scales, quadrant):
+            nc.sync.dma_start(
+                out=plane[32 * quadrant : 32 * quadrant + 4, :, :].bitcast(I32),
+                in_=scales[:, span(quadrant, 4), :].rearrange("g r n -> r g n").bitcast(I32),
+            )
+
+        def load_words(halves, words, half):
+            nc.sync.dma_start(
+                out=halves[half][:].bitcast(I32),
+                in_=words[:, :, span(half, 2 * GROUP)].rearrange("g p n -> p g n").bitcast(I32),
+            )
+
+        def load_l(row_tile):
+            nc.sync.dma_start(out=l_rows[row_tile][:], in_=lin[span(row_tile, P), :])
+
+        def load_m(gb, gc):
+            nc.sync.dma_start(
+                out=m_raw[2 * gb + gc][:],
+                in_=m1[span(gb, GROUP), span(gc, GROUP)].rearrange("(p j) c -> p j c", j=PACK),
+            )
+
+        def load_w(gc):
+            nc.sync.dma_start(out=w_rows[gc][:], in_=w[span(gc, GROUP), :].rearrange("(p t) a -> p t a", t=PACK))
+
+        def warm_up():
+            nc.vector.memset(warm_in[:].bitcast(I32), 0)
+            nc.vector.quantize_mx(out=warm_codes[:].bitcast(FP8X4), scales=warm_scale[:], in_=warm_in[:])
+            bank = turn_pool.tile([P, GROUP], F32, name="turn")
+            for repeat in range(WARM_PASSES):
+                nc.tensor.matmul_mx(
+                    out=bank[:],
+                    lhsT=u_half[0][:, 0, span(0, 2 * P)].bitcast(FP4X4),
+                    lhsT_scale=warm_scale[:, span(0, P)],
+                    rhs=u_half[0][:, 1, :].bitcast(FP4X4),
+                    rhs_scale=warm_scale[:],
+                    start=True,
+                    stop=True,
+                )
+
+        def make_p_rows(row_tile):
+            half, within = divmod(row_tile, GROUP // P)
+            for gb in range(2):
+                bank = sum_pool.tile([P, GROUP], F32, name="sums")
+                for gk in range(2):
                     nc.tensor.matmul_mx(
                         out=bank[:],
-                        lhsT=u_sb[a // 4][:, g, 256 * (a % 4) : 256 * (a % 4) + 256].bitcast(FP4X4),
-                        lhsT_scale=uv_sc[:, 0, g, 128 * a : 128 * a + 128],
-                        rhs=v_sb[h][:, g, :].bitcast(FP4X4),
-                        rhs_scale=uv_sc[:, 1, g, 512 * h : 512 * h + 512],
-                        start=(g == 0), stop=(g == 1))
-            elif name.startswith("ad"):
-                a, h = int(name[2]), int(name[3])
-                cols = slice(512 * h, 512 * h + 512)
+                        lhsT=u_half[half][:, gk, span(within, 2 * P)].bitcast(FP4X4),
+                        lhsT_scale=u_scale[:, gk, span(row_tile, P)],
+                        rhs=v_half[gb][:, gk, :].bitcast(FP4X4),
+                        rhs_scale=v_scale[:, gk, span(gb, GROUP)],
+                        start=(gk == 0),
+                        stop=(gk == 1),
+                    )
                 nc.vector.tensor_tensor(
-                    out=p_nat[a][:, cols].rearrange("a (u q e) -> a u q e", u=2, e=2),
-                    in0=banks["s1_%d%d" % (a, h)][:].rearrange("a (q u e) -> a u q e", u=2, e=2),
-                    in1=l_sb[a][:, cols].rearrange("a (q u e) -> a u q e", u=2, e=2),
-                    op=ALU.add)
-            elif name.startswith("tr"):
-                a = int(name[2])
-                bank = turn_pool.tile([128, 4, 128], F32, name="turn")
-                banks[name] = bank
-                words = p_nat[a][:].bitcast(F32)
-                for s in range(4):
-                    nc.tensor.transpose(bank[:, s, :], words[:, 128 * s : 128 * s + 128], ident[:])
-            elif name.startswith("cp"):
-                a = int(name[2])
+                    out=p_rows[row_tile][:, span(gb, GROUP)].rearrange("a (u q e) -> a u q e", u=2, e=2),
+                    in0=bank[:].rearrange("a (q u e) -> a u q e", u=2, e=2),
+                    in1=l_rows[row_tile][:, span(gb, GROUP)].rearrange("a (q u e) -> a u q e", u=2, e=2),
+                    op=ALU.add,
+                )
+
+        def turn_p(block):
+            for within in range(BLOCK // P):
+                words = p_rows[block * (BLOCK // P) + within][:].bitcast(F32)
+                bank = turn_pool.tile([P, GROUP], F32, name="turn")
+                for piece in range(4):
+                    nc.tensor.transpose(bank[:, span(piece, P)], words[:, span(piece, P)], ident[:])
                 nc.scalar.copy(
-                    out=p_t[a // 2][:].bitcast(F32).rearrange("p (k a u) -> p k a u", k=2, u=2)[:, :, 128 * (a % 2) : 128 * (a % 2) + 128, :],
-                    in_=banks["tr%d" % a][:].rearrange("p (k u) a -> p k a u", k=2))
-            elif name.startswith("qP"):
-                i = int(name[2])
-                nc.vector.quantize_mx(
-                    out=p_codes[i][:].rearrange("p k a -> p (k a)").bitcast(FP8X4),
-                    scales=p_sc[i][:].rearrange("p k a -> p (k a)"), in_=p_t[i][:])
-            elif name.startswith("s2_"):
-                i, g, b = int(name[3]), int(name[4]), int(name[5])
-                bank = acc_pool.tile([128, 512], F32, name="acc")
-                banks[name] = bank
-                for tt in range(2):
-                    t = 2 * b + tt
-                    for k in range(2):
-                        nc.tensor.matmul_mx(
-                            out=bank[:, 256 * tt : 256 * tt + 256],
-                            lhsT=m_codes[2 * k + g][:, 128 * t : 128 * t + 128].bitcast(FP8X4),
-                            lhsT_scale=m_sc[2 * k + g][:, 128 * t : 128 * t + 128],
-                            rhs=p_codes[i][:, k, :].bitcast(FP8X4),
-                            rhs_scale=p_sc[i][:, k, :],
-                            start=(k == 0), stop=(k == 1))
-            elif name.startswith("mu"):
-                i, g, b = int(name[2]), int(name[3]), int(name[4])
-                nc.vector.scalar_tensor_tensor(
-                    out=y_sb[2 * i + g][:, 2 * b : 2 * b + 2, :],
-                    in0=banks["s2_%d%d%d" % (i, g, b)][:].rearrange("p (t a) -> p t a", t=2),
-                    scalar=COEF,
-                    in1=w_sb[2 * g + i // 2][:, 2 * b : 2 * b + 2, 256 * (i % 2) : 256 * (i % 2) + 256],
-                    op0=ALU.mult, op1=ALU.mult)
-            elif name.startswith("iY"):
-                i, g = int(name[2]), int(name[3])
-                move(name,
-                     y_int[2 * i + g][:].rearrange("p (c i t) -> p c t i", i=4, t=4),
-                     y_sb[2 * i + g][:].rearrange("p t (c i) -> p c t i", i=4))
-            elif name.startswith("qY"):
-                i, g = int(name[2]), int(name[3])
-                nc.vector.quantize_mx(
-                    out=y_codes[i][:, g, :].bitcast(FP8X4),
-                    scales=y_sc[:, g, 256 * i : 256 * i + 256], in_=y_int[2 * i + g][:])
-            elif name.startswith("sy"):
-                i, g = int(name[2]), int(name[3])
-                nc.sync.dma_start(
-                    out=out_0[512 * g : 512 * g + 512, 256 * i : 256 * i + 256].rearrange("(p t) a -> p t a", t=4),
-                    in_=y_sb[2 * i + g][:])
-            elif name.startswith("sq"):
-                i = int(name[2])
-                nc.sync.dma_start(
-                    out=out_1.rearrange("g p m t -> p g (m t)")[:, :, 1024 * i : 1024 * i + 1024].bitcast(I32),
-                    in_=y_codes[i][:].bitcast(I32))
-            elif name.startswith("ss"):
-                q = int(name[2])
-                nc.sync.dma_start(
-                    out=out_2[:, 4 * q : 4 * q + 4, :].rearrange("g r n -> r g n").bitcast(I32),
-                    in_=y_sc[32 * q : 32 * q + 4, :, :].bitcast(I32))
-            else:
-                raise ValueError(name)
+                    out=p_inter[block][:].bitcast(F32).rearrange("p (g a u) -> p g a u", g=2, u=2)[:, :, span(within, P), :],
+                    in_=bank[:].rearrange("p (g u a) -> p g a u", g=2, u=2),
+                )
+
+        def quantize_p(block):
+            nc.vector.quantize_mx(
+                out=p_codes[block][:].rearrange("p g a -> p (g a)").bitcast(FP8X4),
+                scales=p_scale[block][:].rearrange("p g a -> p (g a)"),
+                in_=p_inter[block][:],
+            )
+
+        def quantize_m(gb, gc):
+            quarter = 2 * gb + gc
+            nc.scalar.copy(
+                out=m_inter[quarter][:].rearrange("p (t m j) -> p m j t", t=PACK, j=PACK),
+                in_=m_raw[quarter][:].rearrange("p j (m t) -> p m j t", t=PACK),
+            )
+            nc.vector.quantize_mx(
+                out=m_codes[quarter][:].bitcast(FP8X4), scales=m_scale[quarter][:], in_=m_inter[quarter][:]
+            )
+
+        def make_y(gc, pair, block):
+            bank = sum_pool.tile([P, GROUP], F32, name="sums")
+            for within in range(2):
+                t = 2 * pair + within
+                for gb in range(2):
+                    nc.tensor.matmul_mx(
+                        out=bank[:, span(within, BLOCK)],
+                        lhsT=m_codes[2 * gb + gc][:, span(t, P)].bitcast(FP8X4),
+                        lhsT_scale=m_scale[2 * gb + gc][:, span(t, P)],
+                        rhs=p_codes[block][:, gb, :].bitcast(FP8X4),
+                        rhs_scale=p_scale[block][:, gb, :],
+                        start=(gb == 0),
+                        stop=(gb == 1),
+                    )
+            nc.vector.scalar_tensor_tensor(
+                out=y_rows[gc][:, span(pair, 2), span(block, BLOCK)],
+                in0=bank[:].rearrange("p (t a) -> p t a", t=2),
+                scalar=COEF,
+                in1=w_rows[gc][:, span(pair, 2), span(block, BLOCK)],
+                op0=ALU.mult,
+                op1=ALU.mult,
+            )
+
+        def interleave_y(copy, gc, cols):
+            copy(
+                out=y_inter[gc][:, PACK * cols.start : PACK * cols.stop].rearrange("p (n i t) -> p n t i", i=4, t=PACK),
+                in_=y_rows[gc][:, :, cols].rearrange("p t (n i) -> p n t i", i=4),
+            )
+
+        def quantize_y(gc, half):
+            nc.vector.quantize_mx(
+                out=y_codes[gc][:, span(half, GROUP)].bitcast(FP8X4),
+                scales=y_scale[:, gc, span(half, GROUP)],
+                in_=y_inter[gc][:, span(half, PACK * GROUP)],
+            )
+
+        def store_y(gc, pair, cols):
+            rows = out_0[span(gc, GROUP), :].rearrange("(p t) a -> p t a", t=PACK)
+            nc.sync.dma_start(out=rows[:, span(pair, 2), cols], in_=y_rows[gc][:, span(pair, 2), cols])
+
+        def store_codes(gc, cols):
+            nc.sync.dma_start(
+                out=out_1[gc].rearrange("p m t -> p (m t)")[:, PACK * cols.start : PACK * cols.stop].bitcast(I32),
+                in_=y_codes[gc][:, cols].bitcast(I32),
+            )
+
+        def store_scale_rows(quadrant):
+            nc.sync.dma_start(
+                out=out_2[:, span(quadrant, 4), :].rearrange("g r n -> r g n").bitcast(I32),
+                in_=y_scale[32 * quadrant : 32 * quadrant + 4, :, :].bitcast(I32),
+            )
+
+        whole = span(0, D)
+        on_scalar, on_vector = nc.scalar.copy, nc.vector.tensor_copy
 
         with tc.manual_schedule():
-            for name in ORDER:
-                emit(name)
+            for plane in (u_scale, v_scale):
+                nc.vector.memset(plane[:].rearrange("p g n -> p (g n)").bitcast(I32), 0)
+            make_identity(nc, ident[:])
+
+            load_words(u_half, u_words, 0)
+            for quadrant in range(4):
+                load_scale_rows(u_scale, u_scales, quadrant)
+            for quadrant in (0, 1):
+                load_scale_rows(v_scale, v_scales, quadrant)
+            load_words(v_half, v_words, 0)
+            for quadrant in (2, 3):
+                load_scale_rows(v_scale, v_scales, quadrant)
+            load_l(0)
+            load_words(v_half, v_words, 1)
+            load_m(0, 0)
+            for row_tile in (1, 2, 3):
+                load_l(row_tile)
+            load_m(1, 0)
+            load_words(u_half, u_words, 1)
+            load_l(4)
+            load_m(0, 1)
+            for row_tile in (5, 6, 7):
+                load_l(row_tile)
+            load_w(0)
+            load_m(1, 1)
+            load_w(1)
+
+            warm_up()
+            for row_tile in (0, 1, 2):
+                make_p_rows(row_tile)
+            quantize_m(0, 0)
+            turn_p(0)
+            make_p_rows(3)
+            quantize_p(0)
+            make_p_rows(4)
+            quantize_m(1, 0)
+            turn_p(1)
+            for row_tile in (5, 6):
+                make_p_rows(row_tile)
+            quantize_p(1)
+            make_p_rows(7)
+            quantize_m(0, 1)
+            turn_p(2)
+            quantize_p(2)
+
+            make_y(0, 0, 0)
+            turn_p(3)
+            make_y(0, 0, 1)
+            store_y(0, 0, span(0, GROUP))
+            quantize_p(3)
+            make_y(0, 0, 2)
+            make_y(0, 1, 0)
+            make_y(0, 0, 3)
+            store_y(0, 0, span(1, GROUP))
+            quantize_m(1, 1)
+            interleave_y(on_scalar, 0, span(0, BLOCK))
+            for block in (1, 2, 3):
+                make_y(0, 1, block)
+                interleave_y(on_scalar, 0, span(block, BLOCK))
+            store_y(0, 1, whole)
+
+            for block in range(4):
+                make_y(1, 0, block)
+            store_y(1, 0, whole)
+            for block in (0, 1):
+                make_y(1, 1, block)
+                interleave_y(on_scalar, 1, span(block, BLOCK))
+                quantize_y(0, block)
+            store_codes(0, whole)
+            make_y(1, 1, 2)
+            interleave_y(on_scalar, 1, span(4, P))
+            make_y(1, 1, 3)
+            store_y(1, 1, whole)
+            interleave_y(on_vector, 1, span(5, P))
+            interleave_y(on_vector, 1, span(6, P, 2))
+            quantize_y(1, 0)
+            store_codes(1, span(0, GROUP))
+            quantize_y(1, 1)
+            for quadrant in range(4):
+                store_scale_rows(quadrant)
+            store_codes(1, span(1, GROUP))

from contextlib import ExitStack

import concourse.mybir as mybir
from concourse.masks import make_identity

F32 = mybir.dt.float32
BF16 = mybir.dt.bfloat16
I32 = mybir.dt.int32
U32 = mybir.dt.uint32
U8 = mybir.dt.uint8
FP8X4 = mybir.dt.float8_e4m3fn_x4
FP4X4 = mybir.dt.float4_e2m1fn_x4
ALU = mybir.AluOpType

D = 1024
P = 128
PACK = 4
GROUP = P * PACK
BLOCK = 256
COEF = 0.25
FLOPS = 2 * 2 * D * D * D

SUM_BANKS = 6
TURN_BANKS = 2
WARM_PASSES = 4


def tile_notears_acyclicity_gradient_k5_kernel(
    tc, u_words, u_scales, v_words, v_scales, lin, m1, w, out_0, out_1, out_2
):
    nc = tc.nc
    with ExitStack() as ctx:
        sbuf = ctx.enter_context(tc.tile_pool(name="sbuf", bufs=1))
        sum_pool = ctx.enter_context(tc.psum_pool(name="sums", bufs=SUM_BANKS))
        turn_pool = ctx.enter_context(tc.psum_pool(name="turns", bufs=TURN_BANKS))

        def tile(name, shape, dtype):
            return sbuf.tile(shape, dtype, name=name, align_bytes=64)

        def tiles(name, count, shape, dtype):
            return [tile("%s%d" % (name, j), shape, dtype) for j in range(count)]

        ident = tile("ident", [P, P], F32)
        u_scale = tile("u_scale", [P, 2, D], U8)
        v_scale = tile("v_scale", [P, 2, D], U8)
        u_half = tiles("u_half", 2, [P, 2, 2 * GROUP], U8)
        v_half = tiles("v_half", 2, [P, 2, 2 * GROUP], U8)
        warm_in = tile("warm_in", [P, PACK * GROUP], BF16)
        warm_codes = tile("warm_codes", [P, GROUP], U32)
        warm_scale = tile("warm_scale", [P, GROUP], U8)
        l_rows = tiles("l_rows", D // P, [P, D], BF16)
        p_rows = tiles("p_rows", D // P, [P, D], BF16)
        p_inter = tiles("p_inter", D // BLOCK, [P, 2 * BLOCK * PACK], BF16)
        p_codes = tiles("p_codes", D // BLOCK, [P, 2, BLOCK], U32)
        p_scale = tiles("p_scale", D // BLOCK, [P, 2, BLOCK], U8)
        m_raw = tiles("m_raw", 4, [P, PACK, GROUP], BF16)
        m_inter = tiles("m_inter", 4, [P, PACK * GROUP], BF16)
        m_codes = tiles("m_codes", 4, [P, GROUP], U32)
        m_scale = tiles("m_scale", 4, [P, GROUP], U8)
        w_rows = tiles("w_rows", 2, [P, PACK, D], BF16)
        y_rows = tiles("y_rows", 2, [P, PACK, D], F32)
        y_inter = tiles("y_inter", 2, [P, PACK * D], BF16)
        y_codes = tiles("y_codes", 2, [P, D], U32)
        y_scale = tile("y_scale", [P, 2, D], U8)

        def span(index, width, count=1):
            return slice(index * width, (index + count) * width)

        def load_scale_rows(plane, scales, quadrant):
            nc.sync.dma_start(
                out=plane[32 * quadrant : 32 * quadrant + 4, :, :].bitcast(I32),
                in_=scales[:, span(quadrant, 4), :].rearrange("g r n -> r g n").bitcast(I32),
            )

        def load_words(halves, words, half):
            nc.sync.dma_start(
                out=halves[half][:].bitcast(I32),
                in_=words[:, :, span(half, 2 * GROUP)].rearrange("g p n -> p g n").bitcast(I32),
            )

        def load_l(row_tile):
            nc.sync.dma_start(out=l_rows[row_tile][:], in_=lin[span(row_tile, P), :])

        def load_m(gb, gc):
            nc.sync.dma_start(
                out=m_raw[2 * gb + gc][:],
                in_=m1[span(gb, GROUP), span(gc, GROUP)].rearrange("(p j) c -> p j c", j=PACK),
            )

        def load_w(gc):
            nc.sync.dma_start(out=w_rows[gc][:], in_=w[span(gc, GROUP), :].rearrange("(p t) a -> p t a", t=PACK))

        def warm_up():
            nc.vector.memset(warm_in[:].bitcast(I32), 0)
            nc.vector.quantize_mx(out=warm_codes[:].bitcast(FP8X4), scales=warm_scale[:], in_=warm_in[:])
            bank = turn_pool.tile([P, GROUP], F32, name="turn")
            for repeat in range(WARM_PASSES):
                nc.tensor.matmul_mx(
                    out=bank[:],
                    lhsT=u_half[0][:, 0, span(0, 2 * P)].bitcast(FP4X4),
                    lhsT_scale=warm_scale[:, span(0, P)],
                    rhs=u_half[0][:, 1, :].bitcast(FP4X4),
                    rhs_scale=warm_scale[:],
                    start=True,
                    stop=True,
                )

        def make_p_rows(row_tile):
            half, within = divmod(row_tile, GROUP // P)
            for gb in range(2):
                bank = sum_pool.tile([P, GROUP], F32, name="sums")
                for gk in range(2):
                    nc.tensor.matmul_mx(
                        out=bank[:],
                        lhsT=u_half[half][:, gk, span(within, 2 * P)].bitcast(FP4X4),
                        lhsT_scale=u_scale[:, gk, span(row_tile, P)],
                        rhs=v_half[gb][:, gk, :].bitcast(FP4X4),
                        rhs_scale=v_scale[:, gk, span(gb, GROUP)],
                        start=(gk == 0),
                        stop=(gk == 1),
                    )
                nc.vector.tensor_tensor(
                    out=p_rows[row_tile][:, span(gb, GROUP)].rearrange("a (u q e) -> a u q e", u=2, e=2),
                    in0=bank[:].rearrange("a (q u e) -> a u q e", u=2, e=2),
                    in1=l_rows[row_tile][:, span(gb, GROUP)].rearrange("a (q u e) -> a u q e", u=2, e=2),
                    op=ALU.add,
                )

        def turn_p(block):
            for within in range(BLOCK // P):
                words = p_rows[block * (BLOCK // P) + within][:].bitcast(F32)
                bank = turn_pool.tile([P, GROUP], F32, name="turn")
                for piece in range(4):
                    nc.tensor.transpose(bank[:, span(piece, P)], words[:, span(piece, P)], ident[:])
                nc.scalar.copy(
                    out=p_inter[block][:].bitcast(F32).rearrange("p (g a u) -> p g a u", g=2, u=2)[:, :, span(within, P), :],
                    in_=bank[:].rearrange("p (g u a) -> p g a u", g=2, u=2),
                )

        def quantize_p(block):
            nc.vector.quantize_mx(
                out=p_codes[block][:].rearrange("p g a -> p (g a)").bitcast(FP8X4),
                scales=p_scale[block][:].rearrange("p g a -> p (g a)"),
                in_=p_inter[block][:],
            )

        def quantize_m(gb, gc):
            quarter = 2 * gb + gc
            nc.scalar.copy(
                out=m_inter[quarter][:].rearrange("p (t m j) -> p m j t", t=PACK, j=PACK),
                in_=m_raw[quarter][:].rearrange("p j (m t) -> p m j t", t=PACK),
            )
            nc.vector.quantize_mx(
                out=m_codes[quarter][:].bitcast(FP8X4), scales=m_scale[quarter][:], in_=m_inter[quarter][:]
            )

        def make_y(gc, pair, block):
            bank = sum_pool.tile([P, GROUP], F32, name="sums")
            for within in range(2):
                t = 2 * pair + within
                for gb in range(2):
                    nc.tensor.matmul_mx(
                        out=bank[:, span(within, BLOCK)],
                        lhsT=m_codes[2 * gb + gc][:, span(t, P)].bitcast(FP8X4),
                        lhsT_scale=m_scale[2 * gb + gc][:, span(t, P)],
                        rhs=p_codes[block][:, gb, :].bitcast(FP8X4),
                        rhs_scale=p_scale[block][:, gb, :],
                        start=(gb == 0),
                        stop=(gb == 1),
                    )
            nc.vector.scalar_tensor_tensor(
                out=y_rows[gc][:, span(pair, 2), span(block, BLOCK)],
                in0=bank[:].rearrange("p (t a) -> p t a", t=2),
                scalar=COEF,
                in1=w_rows[gc][:, span(pair, 2), span(block, BLOCK)],
                op0=ALU.mult,
                op1=ALU.mult,
            )

        def interleave_y(copy, gc, cols):
            copy(
                out=y_inter[gc][:, PACK * cols.start : PACK * cols.stop].rearrange("p (n i t) -> p n t i", i=4, t=PACK),
                in_=y_rows[gc][:, :, cols].rearrange("p t (n i) -> p n t i", i=4),
            )

        def quantize_y(gc, half):
            nc.vector.quantize_mx(
                out=y_codes[gc][:, span(half, GROUP)].bitcast(FP8X4),
                scales=y_scale[:, gc, span(half, GROUP)],
                in_=y_inter[gc][:, span(half, PACK * GROUP)],
            )

        def store_y(gc, pair, cols):
            rows = out_0[span(gc, GROUP), :].rearrange("(p t) a -> p t a", t=PACK)
            nc.sync.dma_start(out=rows[:, span(pair, 2), cols], in_=y_rows[gc][:, span(pair, 2), cols])

        def store_codes(gc, cols):
            nc.sync.dma_start(
                out=out_1[gc].rearrange("p m t -> p (m t)")[:, PACK * cols.start : PACK * cols.stop].bitcast(I32),
                in_=y_codes[gc][:, cols].bitcast(I32),
            )

        def store_scale_rows(quadrant):
            nc.sync.dma_start(
                out=out_2[:, span(quadrant, 4), :].rearrange("g r n -> r g n").bitcast(I32),
                in_=y_scale[32 * quadrant : 32 * quadrant + 4, :, :].bitcast(I32),
            )

        whole = span(0, D)
        on_scalar, on_vector = nc.scalar.copy, nc.vector.tensor_copy

        with tc.manual_schedule():
            for plane in (u_scale, v_scale):
                nc.vector.memset(plane[:].rearrange("p g n -> p (g n)").bitcast(I32), 0)
            make_identity(nc, ident[:])

            load_words(u_half, u_words, 0)
            for quadrant in range(4):
                load_scale_rows(u_scale, u_scales, quadrant)
            for quadrant in (0, 1):
                load_scale_rows(v_scale, v_scales, quadrant)
            load_words(v_half, v_words, 0)
            for quadrant in (2, 3):
                load_scale_rows(v_scale, v_scales, quadrant)
            load_l(0)
            load_words(v_half, v_words, 1)
            load_m(0, 0)
            for row_tile in (1, 2, 3):
                load_l(row_tile)
            load_m(1, 0)
            load_words(u_half, u_words, 1)
            load_l(4)
            load_m(0, 1)
            for row_tile in (5, 6, 7):
                load_l(row_tile)
            load_w(0)
            load_m(1, 1)
            load_w(1)

            warm_up()
            for row_tile in (0, 1, 2):
                make_p_rows(row_tile)
            quantize_m(0, 0)
            turn_p(0)
            make_p_rows(3)
            quantize_p(0)
            make_p_rows(4)
            quantize_m(1, 0)
            turn_p(1)
            for row_tile in (5, 6):
                make_p_rows(row_tile)
            quantize_p(1)
            make_p_rows(7)
            quantize_m(0, 1)
            turn_p(2)
            quantize_p(2)

            make_y(0, 0, 0)
            turn_p(3)
            make_y(0, 0, 1)
            store_y(0, 0, span(0, GROUP))
            quantize_p(3)
            make_y(0, 0, 2)
            make_y(0, 1, 0)
            make_y(0, 0, 3)
            store_y(0, 0, span(1, GROUP))
            quantize_m(1, 1)
            interleave_y(on_scalar, 0, span(0, BLOCK))
            for block in (1, 2, 3):
                make_y(0, 1, block)
                interleave_y(on_scalar, 0, span(block, BLOCK))
            store_y(0, 1, whole)

            for block in range(4):
                make_y(1, 0, block)
            store_y(1, 0, whole)
            for block in (0, 1):
                make_y(1, 1, block)
                interleave_y(on_scalar, 1, span(block, BLOCK))
                quantize_y(0, block)
            store_codes(0, whole)
            make_y(1, 1, 2)
            interleave_y(on_scalar, 1, span(4, P))
            make_y(1, 1, 3)
            store_y(1, 1, whole)
            interleave_y(on_vector, 1, span(5, P))
            interleave_y(on_vector, 1, span(6, P, 2))
            quantize_y(1, 0)
            store_codes(1, span(0, GROUP))
            quantize_y(1, 1)
            for quadrant in range(4):
                store_scale_rows(quadrant)
            store_codes(1, span(1, GROUP))
